import numpy as np
import ml_dtypes


def mxq(x, axis, fmt="e4m3"):
    dtype, down = {"e4m3": (ml_dtypes.float8_e4m3fn, 7), "e5m2": (ml_dtypes.float8_e5m2, 14)}[fmt]
    v = np.moveaxis(np.asarray(x, np.float32).astype(ml_dtypes.bfloat16).astype(np.float64), axis, -1)
    blocks = v.reshape(v.shape[:-1] + (-1, 32))
    amax = np.abs(blocks).max(-1, keepdims=True)
    byte = np.maximum(np.where(amax > 0, np.frexp(amax)[1] - 1 + 127, 0) - down, 1)
    scale = np.exp2(byte - 127.0)
    codes = (blocks / scale).astype(np.float32).astype(dtype).astype(np.float64)
    return np.moveaxis((codes * scale).reshape(v.shape), -1, axis)


WIDE = False


def mx_kscale(k):
    if not WIDE:
        return np.ones(k)
    levels = np.array([10, -10, 5, -5, 0])
    if k % 512:
        return np.exp2(np.random.permutation(np.resize(levels, k // 32))).repeat(32)
    a = np.empty((k // 512, 16))
    for p in range(k // 512):
        a[p, :8] = np.random.permutation(np.resize(levels, 8))
        for g in range(8):
            far = levels[np.abs(levels - a[p, g]) >= 10]
            a[p, g + 8] = far[np.random.randint(len(far))]
    return np.exp2(a.ravel()).repeat(32)


def f64(x):
    return np.asarray(x).astype(np.float64)


def striped(idx):
    return np.tile(idx.reshape(-1, 16).T, (8, 1)).astype(np.uint16)


def unstriped(offs):
    return offs[:16].T.reshape(-1).astype(np.int64)


def striped8(idx):
    return np.concatenate([x.reshape(-1, 16).T for x in idx]).astype(np.uint16)


def runs(offs, k):
    lists = np.stack([offs[16 * r : 16 * r + 16].T.reshape(-1) for r in range(8)]).astype(np.int64)
    return lists[np.arange(k) % 512 // 64]


def pack_weight(w):
    k, n = w.shape
    w = f64(np.asarray(w, np.float32).astype(ml_dtypes.bfloat16)).reshape(k // 32, 32, n)
    amax = np.abs(w).max(1)
    byte = np.clip(np.where(amax > 0, np.frexp(amax)[1] - 1 + 127 - 7, 1), 1, 254)
    scaled = (w * np.exp2(127.0 - byte)[:, None, :]).reshape(k, n).astype(np.float32)
    words = np.ascontiguousarray(scaled.reshape(k // 512, 128, 4, n).transpose(0, 1, 3, 2)).astype(ml_dtypes.float8_e4m3fn).view(np.uint8)
    return words, np.ascontiguousarray(byte.astype(np.uint8).reshape(k // 512, 16, n))


def unpack_weight(words, scales):
    g, p, n, _ = words.shape
    vals = np.ascontiguousarray(words).view(ml_dtypes.float8_e4m3fn).astype(np.float64) * np.repeat(np.exp2(scales.astype(np.float64) - 127.0), 8, axis=1)[..., None]
    return vals.transpose(0, 1, 3, 2).reshape(g * 512, n)


K, T, S, N, H = 512, 2048, 512, 512, 512


def setup_inputs():
    n = np.random.standard_normal
    s = mx_kscale(K)[:, None]
    u = mx_kscale(H)
    packed_xT = pack_weight(n((K, T)) * s)
    return {
        "x_words": packed_xT[0],
        "x_scales": packed_xT[1],
        "w1": (n((K, H)) / np.sqrt(K) / s).astype(np.float32),
        "gn": (np.random.uniform(0.5, 1.5, (H, 1)) * u[:, None]).astype(np.float32),
        "w2": (n((H, N)) / np.sqrt(H) / u[:, None]).astype(np.float32),
        "gm": (np.random.uniform(0.5, 1.5, (H, 1)) * u[:, None]).astype(np.float32),
        "w3": (n((H, N)) / np.sqrt(H) / u[:, None]).astype(np.float32),
        "offs": striped(np.random.permutation(T)[:S]),
        "n1": striped8(np.stack([np.random.permutation(S) for _ in range(8)])),
        "n2": striped8(np.stack([np.random.permutation(S) for _ in range(8)])),
        "n3": striped8(np.stack([np.random.permutation(S) for _ in range(8)])),
        "n4": striped8(np.stack([np.random.permutation(S) for _ in range(8)])),
        "n5": striped8(np.stack([np.random.permutation(S) for _ in range(8)])),
        "n6": striped8(np.stack([np.random.permutation(S) for _ in range(8)])),
    }


def reference(x_words, x_scales, w1, gn, w2, gm, w3, offs, n1, n2, n3, n4, n5, n6):
    xq = unpack_weight(x_words, x_scales)[:, unstriped(offs)]
    y = mxq(f64(w1), 0, "e4m3").T @ xq
    z = f64(gn) * ((y - (y[np.arange(H)[:, None], runs(n1, H)])) / (np.abs(y[np.arange(H)[:, None], runs(n2, H)] - y) + 0.5))
    a = mxq(f64(w2), 0, "e4m3").T @ mxq(z, 0, "e4m3")
    z2 = f64(gm) * (y * (y[np.arange(H)[:, None], runs(n3, H)] - (y[np.arange(H)[:, None], runs(n4, H)])))
    b = mxq(f64(w3), 0, "e4m3").T @ mxq(z2, 0, "e4m3")
    return np.maximum(a, b[np.arange(N)[:, None], runs(n6, N)]) - (np.minimum(a[np.arange(N)[:, None], runs(n5, N)], b))

@@ -1,0 +1,198 @@
+from contextlib import ExitStack
+
+import concourse.mybir as mybir
+
+K, T, S, N, H = 512, 2048, 512, 512, 512
+FLOPS = 2 * S * (K * H + 2 * H * N)
+
+F32 = mybir.dt.float32
+BF16 = mybir.dt.bfloat16
+I32 = mybir.dt.int32
+U32 = mybir.dt.uint32
+U16 = mybir.dt.uint16
+U8 = mybir.dt.uint8
+FP8X4 = mybir.dt.float8_e4m3fn_x4
+ALU = mybir.AluOpType
+ACT = mybir.ActivationFunctionType
+
+P = 128
+PACK = 4
+
+
+def tile_picked_forkmaxbfracwind_none_p_kernel(
+    tc, x_words, x_scales, w1, gn, w2, gm, w3, offs, n1, n2, n3, n4, n5, n6, out
+):
+    nc = tc.nc
+    with ExitStack() as ctx:
+        lists = ctx.enter_context(tc.tile_pool(name="lists", bufs=1))
+        keep = ctx.enter_context(tc.tile_pool(name="keep", bufs=1))
+        psum = ctx.enter_context(tc.psum_pool(name="psum", bufs=1))
+
+        def load_list(name, src):
+            tile = lists.tile([P, S // 16], U16, name=name)
+            nc.sync.dma_start(tile[:], src)
+            return tile
+
+        def load_weight(name, src, tag):
+            raw = keep.tile([P, PACK, H], F32, name=name, tag=tag, align_bytes=64)
+            nc.sync.dma_start(raw[:], src.rearrange("(p j) c -> p j c", j=PACK))
+            return raw
+
+        def deal_weight(name, raw, shares):
+            grouped = keep.tile([P, PACK * H], BF16, name=name, align_bytes=64)
+            dst = grouped[:].rearrange("p (t m j) -> p m j t", t=PACK, j=PACK)
+            src = raw[:].rearrange("p j (m t) -> p m j t", t=PACK)
+            for engine_copy, lo, hi in shares:
+                engine_copy(out=dst[:, lo:hi], in_=src[:, lo:hi])
+            return grouped
+
+        def quantise(name, grouped):
+            codes = keep.tile([P, S], U32, name=name + "_codes", align_bytes=64)
+            scales = keep.tile([P, S], U8, name=name + "_scales", align_bytes=64)
+            nc.vector.quantize_mx(out=codes[:].bitcast(FP8X4), scales=scales[:], in_=grouped[:])
+            return codes, scales
+
+        def product(bank, weight, t, moving):
+            cols = slice(t * P, (t + 1) * P)
+            nc.tensor.matmul_mx(
+                out=bank[:],
+                lhsT=weight[0][:, cols].bitcast(FP8X4),
+                lhsT_scale=weight[1][:, cols],
+                rhs=moving[0][:].bitcast(FP8X4),
+                rhs_scale=moving[1][:],
+                start=True,
+                stop=True,
+            )
+
+        def interleave(name, planes, tag):
+            grouped = keep.tile([P, PACK * S], BF16, name=name, tag=tag, align_bytes=64)
+            nc.scalar.copy(
+                out=grouped[:].rearrange("p (c i t) -> p c t i", i=4, t=PACK),
+                in_=planes[:].rearrange("p t (c i) -> p c t i", i=4),
+            )
+            return grouped
+
+        xs = keep.tile([P, T], U8, name="xs", align_bytes=64)
+        nc.vector.memset(xs[:].bitcast(I32), 0)
+        offs_t = load_list("offs_t", offs)
+        for q in range(4):
+            nc.scalar.dma_start(
+                xs[32 * q : 32 * q + 4, :].bitcast(I32), x_scales[0, 4 * q : 4 * q + 4, :].bitcast(I32)
+            )
+        n4_t = load_list("n4_t", n4)
+        n2_t = load_list("n2_t", n2)
+        n3_t = load_list("n3_t", n3)
+        n1_t = load_list("n1_t", n1)
+        w1_raw = load_weight("w1_raw", w1, "w1_raw")
+        xw = keep.tile([P, T], I32, name="xw", tag="big", align_bytes=64)
+        nc.sync.dma_start(xw[:], x_words[0].rearrange("p n r -> p (n r)").bitcast(I32))
+        n6_t = load_list("n6_t", n6)
+        n5_t = load_list("n5_t", n5)
+        gm_t = keep.tile([P, PACK], F32, name="gm_t")
+        nc.gpsimd.dma_start(gm_t[:], gm.rearrange("(p t) o -> p (t o)", t=PACK))
+        gn_t = keep.tile([P, PACK], F32, name="gn_t")
+        nc.gpsimd.dma_start(gn_t[:], gn.rearrange("(p t) o -> p (t o)", t=PACK))
+
+        half = keep.tile([P, 1], F32, name="half")
+        nc.vector.memset(half[:], 0.5)
+        win = [keep.tile([P, 2 * S], F32, name=f"win{t}") for t in range(PACK)]
+        bwin = [keep.tile([P, 2 * S], F32, name=f"bwin{t}") for t in range(PACK)]
+        for t in range(PACK):
+            nc.vector.memset(win[t][:, S:], 0.0)
+
+        xq_scales = keep.tile([P, S], U8, name="xq_scales", align_bytes=64)
+        nc.vector.tensor_copy(xq_scales[:], xs[:].indirect(offs_t[:]))
+        w1_q = quantise("w1", deal_weight("w1_bf", w1_raw, [(nc.scalar.copy, 0, 64), (nc.vector.tensor_copy, 64, P)]))
+        xq_words = keep.tile([P, S], U32, name="xq_words", align_bytes=64)
+        nc.vector.tensor_copy(xq_words[:], xw[:].bitcast(U32).indirect(offs_t[:]))
+        w3_raw = load_weight("w3_raw", w3, "big")
+
+        y_plain = [bwin[t][:, S:] for t in range(PACK)]
+        for t in range(PACK):
+            bank = psum.tile([P, S], F32, name=f"y_bank{t}", tag=f"first{t}")
+            product(bank, w1_q, t, (xq_words, xq_scales))
+            nc.scalar.copy(win[t][:, :S], bank[:])
+            nc.scalar.copy(y_plain[t], bank[:])
+
+        neg_gn = keep.tile([P, PACK], F32, name="neg_gn")
+        nc.vector.tensor_scalar(neg_gn[:], gn_t[:], -1.0, None, ALU.mult)
+
+        g4 = keep.tile([P, PACK, S], F32, name="g4")
+        d3 = keep.tile([P, PACK, S], F32, name="d3")
+        recip = keep.tile([P, PACK, S], F32, name="recip")
+        z2 = keep.tile([P, PACK, S], F32, name="z2")
+
+        def z2_product(t):
+            nc.vector.scalar_tensor_tensor(z2[:, t, :], d3[:, t, :], gm_t[:, t : t + 1], y_plain[t], ALU.mult, ALU.mult)
+
+        for t in range(PACK):
+            nc.vector.tensor_copy(g4[:, t, :], win[t][:].indirect(n4_t[:]))
+            nc.vector.tensor_tensor(recip[:, t, :], win[t][:].indirect(n2_t[:]), y_plain[t], ALU.subtract)
+            nc.vector.tensor_tensor(d3[:, t, :], win[t][:].indirect(n3_t[:]), g4[:, t, :], ALU.subtract)
+            if t > 0:
+                z2_product(t - 1)
+            nc.scalar.activation(recip[:, t, :], recip[:, t, :], ACT.Abs)
+            nc.scalar.activation(recip[:, t, :], recip[:, t, :], ACT.Abs_reciprocal_sqrt, bias=half[:])
+            nc.scalar.activation(recip[:, t, :], recip[:, t, :], ACT.Square)
+            if t == 0:
+                w3_bf = deal_weight("w3_bf", w3_raw, [(nc.scalar.copy, 0, P)])
+                w2_raw = load_weight("w2_raw", w2, "big")
+            if t == 1:
+                w3_q = quantise("w3", w3_bf)
+
+        e1_first = keep.tile([P, 2, S], F32, name="e1_first")
+        nc.vector.tensor_tensor(e1_first[:, 0, :], win[0][:].indirect(n1_t[:]), y_plain[0], ALU.subtract)
+        z2_product(PACK - 1)
+        z2_bf = interleave("z2_bf", z2, "z2_bf")
+        w2_bf = deal_weight("w2_bf", w2_raw, [(nc.scalar.copy, 0, P)])
+        nc.vector.tensor_tensor(e1_first[:, 1, :], win[1][:].indirect(n1_t[:]), y_plain[1], ALU.subtract)
+
+        z = keep.tile([P, PACK, S], F32, name="z")
+
+        def z_product(t, e1):
+            nc.vector.scalar_tensor_tensor(z[:, t, :], e1, neg_gn[:, t : t + 1], recip[:, t, :], ALU.mult, ALU.mult)
+
+        z_product(0, e1_first[:, 0, :])
+        z2_q = quantise("z2", z2_bf)
+        z_product(1, e1_first[:, 1, :])
+        for t in range(PACK):
+            bank = psum.tile([P, S], F32, name=f"b_bank{t}", tag=f"second{t}")
+            product(bank, w3_q, t, z2_q)
+            nc.scalar.copy(bwin[t][:, :S], bank[:])
+        e1_last = keep.tile([P, 2, S], F32, name="e1_last", tag="z2_bf", align_bytes=64)
+        for t in (2, 3):
+            nc.vector.tensor_tensor(e1_last[:, t - 2, :], win[t][:].indirect(n1_t[:]), y_plain[t], ALU.subtract)
+        z_product(2, e1_last[:, 0, :])
+        w2_q = quantise("w2", w2_bf)
+        z_product(3, e1_last[:, 1, :])
+        z_bf = interleave("z_bf", z, "z_bf")
+
+        g6_first = keep.tile([P, 3, S], F32, name="g6_first")
+        for t in range(3):
+            nc.vector.tensor_copy(g6_first[:, t, :], bwin[t][:].indirect(n6_t[:]))
+        z_q = quantise("z", z_bf)
+        for t in range(PACK):
+            bank = psum.tile([P, S], F32, name=f"a_bank{t}", tag=f"first{t}")
+            product(bank, w2_q, t, z_q)
+            nc.scalar.copy(win[t][:, :S], bank[:])
+        g6_last = keep.tile([P, S], F32, name="g6_last", tag="z_bf", align_bytes=64)
+        nc.vector.tensor_copy(g6_last[:], bwin[3][:].indirect(n6_t[:]))
+        g6 = [g6_first[:, 0, :], g6_first[:, 1, :], g6_first[:, 2, :], g6_last[:]]
+
+        out_rows = out.rearrange("(p t) j -> p t j", t=PACK)
+        larger = keep.tile([P, PACK, S], F32, name="larger")
+        smaller = keep.tile([P, PACK, S], F32, name="smaller")
+        g5 = keep.tile([P, PACK, S], F32, name="g5")
+
+        def finish(t):
+            res = keep.tile([P, S], F32, name=f"res{t}")
+            nc.vector.tensor_tensor(res[:], larger[:, t, :], smaller[:, t, :], ALU.subtract)
+            nc.sync.dma_start(out_rows[:, t, :], res[:])
+
+        for t in range(PACK):
+            nc.vector.tensor_copy(g5[:, t, :], win[t][:].indirect(n5_t[:]))
+            if t > 0:
+                finish(t - 1)
+            nc.vector.tensor_tensor(smaller[:, t, :], g5[:, t, :], bwin[t][:, :S], ALU.min)
+            nc.vector.tensor_tensor(larger[:, t, :], g6[t], win[t][:, :S], ALU.max)
+        finish(PACK - 1)

@@ -38,60 +38,59 @@ def tile_picked_forkmaxbfracwind_none_p_kernel(
             nc.sync.dma_start(raw[:], src.rearrange("(p j) c -> p j c", j=PACK))
             return raw
 
-        def deal_weight(name, raw, shares):
-            grouped = keep.tile([P, PACK * H], BF16, name=name, align_bytes=64)
+        def deal_weight(grouped, raw, shares):
             dst = grouped[:].rearrange("p (t m j) -> p m j t", t=PACK, j=PACK)
             src = raw[:].rearrange("p j (m t) -> p m j t", t=PACK)
             for engine_copy, lo, hi in shares:
                 engine_copy(out=dst[:, lo:hi], in_=src[:, lo:hi])
-            return grouped
 
-        def quantise(name, grouped):
-            codes = keep.tile([P, S], U32, name=name + "_codes", align_bytes=64)
+        def quantise(name, grouped, tag=None, bufs=1):
+            codes = keep.tile([P, S], U32, name=name + "_codes", tag=tag or name + "_codes", bufs=bufs, align_bytes=64)
             scales = keep.tile([P, S], U8, name=name + "_scales", align_bytes=64)
             nc.vector.quantize_mx(out=codes[:].bitcast(FP8X4), scales=scales[:], in_=grouped[:])
             return codes, scales
 
-        def product(bank, weight, t, moving):
+        def product(bank, weight, t, moving, places=slice(0, S)):
             cols = slice(t * P, (t + 1) * P)
             nc.tensor.matmul_mx(
-                out=bank[:],
+                out=bank[:, places],
                 lhsT=weight[0][:, cols].bitcast(FP8X4),
                 lhsT_scale=weight[1][:, cols],
-                rhs=moving[0][:].bitcast(FP8X4),
-                rhs_scale=moving[1][:],
+                rhs=moving[0][:, places].bitcast(FP8X4),
+                rhs_scale=moving[1][:, places],
                 start=True,
                 stop=True,
             )
 
-        def interleave(name, planes, tag):
-            grouped = keep.tile([P, PACK * S], BF16, name=name, tag=tag, align_bytes=64)
-            nc.scalar.copy(
+        def interleave(grouped, planes, sign):
+            nc.scalar.activation(
                 out=grouped[:].rearrange("p (c i t) -> p c t i", i=4, t=PACK),
                 in_=planes[:].rearrange("p t (c i) -> p c t i", i=4),
+                func=ACT.Copy,
+                scale=sign,
             )
-            return grouped
 
         xs = keep.tile([P, T], U8, name="xs", align_bytes=64)
-        nc.vector.memset(xs[:].bitcast(I32), 0)
+        nc.gpsimd.memset(xs[:, : T // 2].bitcast(I32), 0)
+        nc.vector.memset(xs[:, T // 2 :].bitcast(I32), 0)
+        w1_raw = load_weight("w1_raw", w1, "w1_raw")
         offs_t = load_list("offs_t", offs)
         for q in range(4):
-            nc.scalar.dma_start(
+            nc.sync.dma_start(
                 xs[32 * q : 32 * q + 4, :].bitcast(I32), x_scales[0, 4 * q : 4 * q + 4, :].bitcast(I32)
             )
+        xw = keep.tile([P, T], I32, name="xw", tag="big", align_bytes=64)
+        nc.sync.dma_start(xw[:], x_words[0].rearrange("p n r -> p (n r)").bitcast(I32))
         n4_t = load_list("n4_t", n4)
         n2_t = load_list("n2_t", n2)
         n3_t = load_list("n3_t", n3)
+        gm_t = keep.tile([P, PACK], F32, name="gm_t")
+        nc.sync.dma_start(gm_t[:], gm.rearrange("(p t) o -> p (t o)", t=PACK))
+        gn_t = keep.tile([P, PACK], F32, name="gn_t")
+        nc.sync.dma_start(gn_t[:], gn.rearrange("(p t) o -> p (t o)", t=PACK))
         n1_t = load_list("n1_t", n1)
-        w1_raw = load_weight("w1_raw", w1, "w1_raw")
-        xw = keep.tile([P, T], I32, name="xw", tag="big", align_bytes=64)
-        nc.sync.dma_start(xw[:], x_words[0].rearrange("p n r -> p (n r)").bitcast(I32))
         n6_t = load_list("n6_t", n6)
         n5_t = load_list("n5_t", n5)
-        gm_t = keep.tile([P, PACK], F32, name="gm_t")
-        nc.gpsimd.dma_start(gm_t[:], gm.rearrange("(p t) o -> p (t o)", t=PACK))
-        gn_t = keep.tile([P, PACK], F32, name="gn_t")
-        nc.gpsimd.dma_start(gn_t[:], gn.rearrange("(p t) o -> p (t o)", t=PACK))
 
         half = keep.tile([P, 1], F32, name="half")
         nc.vector.memset(half[:], 0.5)
@@ -102,79 +101,95 @@ def tile_picked_forkmaxbfracwind_none_p_kernel(
 
         xq_scales = keep.tile([P, S], U8, name="xq_scales", align_bytes=64)
         nc.vector.tensor_copy(xq_scales[:], xs[:].indirect(offs_t[:]))
-        w1_q = quantise("w1", deal_weight("w1_bf", w1_raw, [(nc.scalar.copy, 0, 64), (nc.vector.tensor_copy, 64, P)]))
+        w1_bf, w2_bf, w3_bf = [keep.tile([P, PACK * H], BF16, name=f"w{i}_bf", align_bytes=64) for i in (1, 2, 3)]
+        deal_weight(w1_bf, w1_raw, [(nc.scalar.copy, 0, 80), (nc.vector.tensor_copy, 80, P)])
+        w1_q = quantise("w1", w1_bf)
         xq_words = keep.tile([P, S], U32, name="xq_words", align_bytes=64)
-        nc.vector.tensor_copy(xq_words[:], xw[:].bitcast(U32).indirect(offs_t[:]))
-        w3_raw = load_weight("w3_raw", w3, "big")
+        halves = [slice(0, S // 2), slice(S // 2, S)]
+        for cols in halves:
+            nc.vector.tensor_copy(xq_words[:, cols], xw[:].bitcast(U32).indirect(offs_t[:, cols.start // 16 : cols.stop // 16]))
+        w3_raw = load_weight("w3_raw", w3, "w1_raw")
+        w2_raw = load_weight("w2_raw", w2, "big")
 
+        last = PACK - 1
         y_plain = [bwin[t][:, S:] for t in range(PACK)]
+        y_gm = keep.tile([P, last, S], F32, name="y_gm")
+        early_bank = psum.tile([P, S], F32, name="early_bank", tag="second0")
         for t in range(PACK):
             bank = psum.tile([P, S], F32, name=f"y_bank{t}", tag=f"first{t}")
-            product(bank, w1_q, t, (xq_words, xq_scales))
-            nc.scalar.copy(win[t][:, :S], bank[:])
-            nc.scalar.copy(y_plain[t], bank[:])
+            parts = [(early_bank, halves[0]), (bank, halves[1])] if t == 0 else [(bank, slice(0, S))]
+            for part, cols in parts:
+                product(part, w1_q, t, (xq_words, xq_scales), cols)
+                nc.scalar.copy(win[t][:, cols], part[:, cols])
+            for part, cols in parts:
+                nc.scalar.copy(y_plain[t][:, cols], part[:, cols])
+            if t < last:
+                for part, cols in parts:
+                    nc.scalar.activation(y_gm[:, t, cols], part[:, cols], ACT.Copy, scale=gm_t[:, t : t + 1])
 
-        neg_gn = keep.tile([P, PACK], F32, name="neg_gn")
-        nc.vector.tensor_scalar(neg_gn[:], gn_t[:], -1.0, None, ALU.mult)
-
-        g4 = keep.tile([P, PACK, S], F32, name="g4")
-        d3 = keep.tile([P, PACK, S], F32, name="d3")
         recip = keep.tile([P, PACK, S], F32, name="recip")
         z2 = keep.tile([P, PACK, S], F32, name="z2")
-
-        def z2_product(t):
-            nc.vector.scalar_tensor_tensor(z2[:, t, :], d3[:, t, :], gm_t[:, t : t + 1], y_plain[t], ALU.mult, ALU.mult)
-
         for t in range(PACK):
-            nc.vector.tensor_copy(g4[:, t, :], win[t][:].indirect(n4_t[:]))
+            g4 = keep.tile([P, S], F32, name=f"g4_{t}", tag="g4", bufs=2)
+            nc.vector.tensor_copy(g4[:], win[t][:].indirect(n4_t[:]))
             nc.vector.tensor_tensor(recip[:, t, :], win[t][:].indirect(n2_t[:]), y_plain[t], ALU.subtract)
-            nc.vector.tensor_tensor(d3[:, t, :], win[t][:].indirect(n3_t[:]), g4[:, t, :], ALU.subtract)
-            if t > 0:
-                z2_product(t - 1)
+            d3 = keep.tile([P, S], F32, name=f"d3_{t}", tag="diff", bufs=2, align_bytes=64)
+            nc.vector.tensor_tensor(d3[:], win[t][:].indirect(n3_t[:]), g4[:], ALU.subtract)
+            if t < last:
+                nc.gpsimd.tensor_tensor(z2[:, t, :], d3[:], y_gm[:, t, :], ALU.mult)
             nc.scalar.activation(recip[:, t, :], recip[:, t, :], ACT.Abs)
             nc.scalar.activation(recip[:, t, :], recip[:, t, :], ACT.Abs_reciprocal_sqrt, bias=half[:])
             nc.scalar.activation(recip[:, t, :], recip[:, t, :], ACT.Square)
             if t == 0:
-                w3_bf = deal_weight("w3_bf", w3_raw, [(nc.scalar.copy, 0, P)])
-                w2_raw = load_weight("w2_raw", w2, "big")
-            if t == 1:
-                w3_q = quantise("w3", w3_bf)
-
-        e1_first = keep.tile([P, 2, S], F32, name="e1_first")
-        nc.vector.tensor_tensor(e1_first[:, 0, :], win[0][:].indirect(n1_t[:]), y_plain[0], ALU.subtract)
-        z2_product(PACK - 1)
-        z2_bf = interleave("z2_bf", z2, "z2_bf")
-        w2_bf = deal_weight("w2_bf", w2_raw, [(nc.scalar.copy, 0, P)])
-        nc.vector.tensor_tensor(e1_first[:, 1, :], win[1][:].indirect(n1_t[:]), y_plain[1], ALU.subtract)
+                deal_weight(w3_bf, w3_raw, [(nc.scalar.copy, 0, P)])
+            if t == 2:
+                deal_weight(w2_bf, w2_raw, [(nc.scalar.copy, 0, P // 2)])
 
         z = keep.tile([P, PACK, S], F32, name="z")
 
-        def z_product(t, e1):
-            nc.vector.scalar_tensor_tensor(z[:, t, :], e1, neg_gn[:, t : t + 1], recip[:, t, :], ALU.mult, ALU.mult)
+        def z_gather(t, e1):
+            nc.vector.tensor_tensor(e1, win[t][:].indirect(n1_t[:]), y_plain[t], ALU.subtract)
 
-        z_product(0, e1_first[:, 0, :])
+        def z_product(t, e1):
+            nc.vector.scalar_tensor_tensor(z[:, t, :], e1, gn_t[:, t : t + 1], recip[:, t, :], ALU.mult, ALU.mult)
+
+        e1 = [keep.tile([P, S], F32, name=f"e1_{t}", tag="diff", bufs=2, align_bytes=64)[:] for t in range(2)]
+        z_gather(0, e1[0])
+        nc.vector.scalar_tensor_tensor(z2[:, last, :], d3[:], gm_t[:, last:], y_plain[last], ALU.mult, ALU.mult)
+        z2_bf = keep.tile([P, PACK * S], BF16, name="z2_bf", tag="z2_bf", align_bytes=64)
+        interleave(z2_bf, z2, 1.0)
+        deal_weight(w2_bf, w2_raw, [(nc.scalar.copy, P // 2, P)])
+        z_gather(1, e1[1])
+        z_product(0, e1[0])
+        w3_q = quantise("w3", w3_bf, "diff", 2)
+        z_product(1, e1[1])
         z2_q = quantise("z2", z2_bf)
-        z_product(1, e1_first[:, 1, :])
+        b_bank = []
         for t in range(PACK):
             bank = psum.tile([P, S], F32, name=f"b_bank{t}", tag=f"second{t}")
             product(bank, w3_q, t, z2_q)
             nc.scalar.copy(bwin[t][:, :S], bank[:])
+            b_bank.append(bank)
         e1_last = keep.tile([P, 2, S], F32, name="e1_last", tag="z2_bf", align_bytes=64)
-        for t in (2, 3):
-            nc.vector.tensor_tensor(e1_last[:, t - 2, :], win[t][:].indirect(n1_t[:]), y_plain[t], ALU.subtract)
-        z_product(2, e1_last[:, 0, :])
+        e1.extend([e1_last[:, 0, :], e1_last[:, 1, :]])
+        z_gather(2, e1[2])
+        z_gather(3, e1[3])
+        z_product(2, e1[2])
+        z_product(3, e1[3])
+        z_bf = keep.tile([P, PACK * S], BF16, name="z_bf", tag="z_bf", align_bytes=64)
+        interleave(z_bf, z, -1.0)
         w2_q = quantise("w2", w2_bf)
-        z_product(3, e1_last[:, 1, :])
-        z_bf = interleave("z_bf", z, "z_bf")
 
         g6_first = keep.tile([P, 3, S], F32, name="g6_first")
         for t in range(3):
             nc.vector.tensor_copy(g6_first[:, t, :], bwin[t][:].indirect(n6_t[:]))
         z_q = quantise("z", z_bf)
+        a_bank = []
         for t in range(PACK):
             bank = psum.tile([P, S], F32, name=f"a_bank{t}", tag=f"first{t}")
             product(bank, w2_q, t, z_q)
             nc.scalar.copy(win[t][:, :S], bank[:])
+            a_bank.append(bank)
         g6_last = keep.tile([P, S], F32, name="g6_last", tag="z_bf", align_bytes=64)
         nc.vector.tensor_copy(g6_last[:], bwin[3][:].indirect(n6_t[:]))
         g6 = [g6_first[:, 0, :], g6_first[:, 1, :], g6_first[:, 2, :], g6_last[:]]
@@ -183,16 +198,18 @@ def tile_picked_forkmaxbfracwind_none_p_kernel(
         larger = keep.tile([P, PACK, S], F32, name="larger")
         smaller = keep.tile([P, PACK, S], F32, name="smaller")
         g5 = keep.tile([P, PACK, S], F32, name="g5")
-
-        def finish(t):
-            res = keep.tile([P, S], F32, name=f"res{t}")
-            nc.vector.tensor_tensor(res[:], larger[:, t, :], smaller[:, t, :], ALU.subtract)
-            nc.sync.dma_start(out_rows[:, t, :], res[:])
-
-        for t in range(PACK):
+        res = keep.tile([P, PACK, S], F32, name="res")
+        for t in range(last):
             nc.vector.tensor_copy(g5[:, t, :], win[t][:].indirect(n5_t[:]))
-            if t > 0:
-                finish(t - 1)
-            nc.vector.tensor_tensor(smaller[:, t, :], g5[:, t, :], bwin[t][:, :S], ALU.min)
-            nc.vector.tensor_tensor(larger[:, t, :], g6[t], win[t][:, :S], ALU.max)
-        finish(PACK - 1)
+            nc.vector.tensor_tensor(larger[:, t, :], g6[t], a_bank[t][:], ALU.max)
+            nc.vector.tensor_tensor(smaller[:, t, :], g5[:, t, :], b_bank[t][:], ALU.min)
+            nc.gpsimd.tensor_tensor(res[:, t, :], larger[:, t, :], smaller[:, t, :], ALU.subtract)
+            nc.sync.dma_start(out_rows[:, t, :], res[:, t, :])
+        nc.vector.tensor_tensor(larger[:, last, :], g6[last], a_bank[last][:], ALU.max)
+        for cols in halves:
+            nc.vector.tensor_copy(g5[:, last, cols], win[last][:].indirect(n5_t[:, cols.start // 16 : cols.stop // 16]))
+        for cols in halves:
+            nc.vector.tensor_tensor(smaller[:, last, cols], g5[:, last, cols], b_bank[last][:, cols], ALU.min)
+        for cols in halves:
+            nc.vector.tensor_tensor(res[:, last, cols], larger[:, last, cols], smaller[:, last, cols], ALU.subtract)
+            nc.sync.dma_start(out_rows[:, last, cols], res[:, last, cols])

@@ -44,8 +44,8 @@ def tile_picked_forkmaxbfracwind_none_p_kernel(
             for engine_copy, lo, hi in shares:
                 engine_copy(out=dst[:, lo:hi], in_=src[:, lo:hi])
 
-        def quantise(name, grouped, tag=None, bufs=1):
-            codes = keep.tile([P, S], U32, name=name + "_codes", tag=tag or name + "_codes", bufs=bufs, align_bytes=64)
+        def quantise(name, grouped, tag=None):
+            codes = keep.tile([P, S], U32, name=name + "_codes", tag=tag or name + "_codes", align_bytes=64)
             scales = keep.tile([P, S], U8, name=name + "_scales", align_bytes=64)
             nc.vector.quantize_mx(out=codes[:].bitcast(FP8X4), scales=scales[:], in_=grouped[:])
             return codes, scales
@@ -70,15 +70,13 @@ def tile_picked_forkmaxbfracwind_none_p_kernel(
                 scale=sign,
             )
 
-        xs = keep.tile([P, T], U8, name="xs", align_bytes=64)
+        xs = keep.tile([P, T], U8, name="xs", tag="xs", align_bytes=64)
         nc.gpsimd.memset(xs[:, : T // 2].bitcast(I32), 0)
         nc.vector.memset(xs[:, T // 2 :].bitcast(I32), 0)
         w1_raw = load_weight("w1_raw", w1, "w1_raw")
         offs_t = load_list("offs_t", offs)
-        for q in range(4):
-            nc.sync.dma_start(
-                xs[32 * q : 32 * q + 4, :].bitcast(I32), x_scales[0, 4 * q : 4 * q + 4, :].bitcast(I32)
-            )
+        for r in range(4):
+            nc.sync.dma_start(xs[r:P:32, :].bitcast(I32), x_scales[0, r:16:4, :].bitcast(I32))
         xw = keep.tile([P, T], I32, name="xw", tag="big", align_bytes=64)
         nc.sync.dma_start(xw[:], x_words[0].rearrange("p n r -> p (n r)").bitcast(I32))
         n4_t = load_list("n4_t", n4)
@@ -94,6 +92,8 @@ def tile_picked_forkmaxbfracwind_none_p_kernel(
 
         half = keep.tile([P, 1], F32, name="half")
         nc.vector.memset(half[:], 0.5)
+        warm = keep.tile([P, 1], F32, name="warm")
+        nc.scalar.activation(warm[:], half[:], ACT.Abs_reciprocal_sqrt)
         win = [keep.tile([P, 2 * S], F32, name=f"win{t}") for t in range(PACK)]
         bwin = [keep.tile([P, 2 * S], F32, name=f"bwin{t}") for t in range(PACK)]
         for t in range(PACK):
@@ -101,9 +101,9 @@ def tile_picked_forkmaxbfracwind_none_p_kernel(
 
         xq_scales = keep.tile([P, S], U8, name="xq_scales", align_bytes=64)
         nc.vector.tensor_copy(xq_scales[:], xs[:].indirect(offs_t[:]))
-        w1_bf, w2_bf, w3_bf = [keep.tile([P, PACK * H], BF16, name=f"w{i}_bf", align_bytes=64) for i in (1, 2, 3)]
+        w1_bf, w3_bf = [keep.tile([P, PACK * H], BF16, name=f"w{i}_bf", align_bytes=64) for i in (1, 3)]
         deal_weight(w1_bf, w1_raw, [(nc.scalar.copy, 0, 80), (nc.vector.tensor_copy, 80, P)])
-        w1_q = quantise("w1", w1_bf)
+        w1_q = quantise("w1", w1_bf, "xs")
         xq_words = keep.tile([P, S], U32, name="xq_words", align_bytes=64)
         halves = [slice(0, S // 2), slice(S // 2, S)]
         for cols in halves:
@@ -127,41 +127,40 @@ def tile_picked_forkmaxbfracwind_none_p_kernel(
                 for part, cols in parts:
                     nc.scalar.activation(y_gm[:, t, cols], part[:, cols], ACT.Copy, scale=gm_t[:, t : t + 1])
 
-        recip = keep.tile([P, PACK, S], F32, name="recip")
-        z2 = keep.tile([P, PACK, S], F32, name="z2")
+        recip = [keep.tile([P, S], F32, name=f"recip{t}")[:] for t in range(PACK)]
+        z2 = keep.tile([P, PACK, S], F32, name="z2", tag="z2", align_bytes=64)
         for t in range(PACK):
             g4 = keep.tile([P, S], F32, name=f"g4_{t}", tag="g4", bufs=2)
             nc.vector.tensor_copy(g4[:], win[t][:].indirect(n4_t[:]))
-            nc.vector.tensor_tensor(recip[:, t, :], win[t][:].indirect(n2_t[:]), y_plain[t], ALU.subtract)
-            d3 = keep.tile([P, S], F32, name=f"d3_{t}", tag="diff", bufs=2, align_bytes=64)
+            nc.vector.tensor_tensor(recip[t], win[t][:].indirect(n2_t[:]), y_plain[t], ALU.subtract)
+            d3 = keep.tile([P, S], F32, name=f"d3_{t}", tag=f"d3_{t}", align_bytes=64)
             nc.vector.tensor_tensor(d3[:], win[t][:].indirect(n3_t[:]), g4[:], ALU.subtract)
             if t < last:
                 nc.gpsimd.tensor_tensor(z2[:, t, :], d3[:], y_gm[:, t, :], ALU.mult)
-            nc.scalar.activation(recip[:, t, :], recip[:, t, :], ACT.Abs)
-            nc.scalar.activation(recip[:, t, :], recip[:, t, :], ACT.Abs_reciprocal_sqrt, bias=half[:])
-            nc.scalar.activation(recip[:, t, :], recip[:, t, :], ACT.Square)
+            nc.scalar.activation(recip[t], recip[t], ACT.Abs)
+            nc.scalar.activation(recip[t], recip[t], ACT.Abs_reciprocal_sqrt, bias=half[:])
+            nc.scalar.activation(recip[t], recip[t], ACT.Square)
             if t == 0:
                 deal_weight(w3_bf, w3_raw, [(nc.scalar.copy, 0, P)])
-            if t == 2:
-                deal_weight(w2_bf, w2_raw, [(nc.scalar.copy, 0, P // 2)])
 
-        z = keep.tile([P, PACK, S], F32, name="z")
+        z = keep.tile([P, PACK, S], F32, name="z", tag="d3_3", align_bytes=64)
 
         def z_gather(t, e1):
             nc.vector.tensor_tensor(e1, win[t][:].indirect(n1_t[:]), y_plain[t], ALU.subtract)
 
         def z_product(t, e1):
-            nc.vector.scalar_tensor_tensor(z[:, t, :], e1, gn_t[:, t : t + 1], recip[:, t, :], ALU.mult, ALU.mult)
+            nc.vector.scalar_tensor_tensor(z[:, t, :], e1, gn_t[:, t : t + 1], recip[t], ALU.mult, ALU.mult)
 
-        e1 = [keep.tile([P, S], F32, name=f"e1_{t}", tag="diff", bufs=2, align_bytes=64)[:] for t in range(2)]
+        e1 = [keep.tile([P, S], F32, name="e1_0", tag="d3_2", align_bytes=64)[:], z[:, 1, :]]
         z_gather(0, e1[0])
         nc.vector.scalar_tensor_tensor(z2[:, last, :], d3[:], gm_t[:, last:], y_plain[last], ALU.mult, ALU.mult)
         z2_bf = keep.tile([P, PACK * S], BF16, name="z2_bf", tag="z2_bf", align_bytes=64)
         interleave(z2_bf, z2, 1.0)
-        deal_weight(w2_bf, w2_raw, [(nc.scalar.copy, P // 2, P)])
-        z_gather(1, e1[1])
+        w2_bf = keep.tile([P, PACK * H], BF16, name="w2_bf", tag="z2", align_bytes=64)
+        deal_weight(w2_bf, w2_raw, [(nc.scalar.copy, 0, P)])
         z_product(0, e1[0])
-        w3_q = quantise("w3", w3_bf, "diff", 2)
+        z_gather(1, e1[1])
+        w3_q = quantise("w3", w3_bf, "d3_2")
         z_product(1, e1[1])
         z2_q = quantise("z2", z2_bf)
         b_bank = []
@@ -184,28 +183,33 @@ def tile_picked_forkmaxbfracwind_none_p_kernel(
         for t in range(3):
             nc.vector.tensor_copy(g6_first[:, t, :], bwin[t][:].indirect(n6_t[:]))
         z_q = quantise("z", z_bf)
-        a_bank = []
-        for t in range(PACK):
-            bank = psum.tile([P, S], F32, name=f"a_bank{t}", tag=f"first{t}")
-            product(bank, w2_q, t, z_q)
-            nc.scalar.copy(win[t][:, :S], bank[:])
-            a_bank.append(bank)
         g6_last = keep.tile([P, S], F32, name="g6_last", tag="z_bf", align_bytes=64)
         nc.vector.tensor_copy(g6_last[:], bwin[3][:].indirect(n6_t[:]))
         g6 = [g6_first[:, 0, :], g6_first[:, 1, :], g6_first[:, 2, :], g6_last[:]]
+        larger = keep.tile([P, PACK, S], F32, name="larger")
+        a_bank = []
+
+        def take_larger(t):
+            nc.vector.tensor_tensor(larger[:, t, :], g6[t], a_bank[t][:], ALU.max)
+
+        for t in range(PACK):
+            bank = psum.tile([P, S], F32, name=f"a_bank{t}", tag=f"first{t}")
+            product(bank, w2_q, t, z_q)
+            a_bank.append(bank)
+            if t == 1:
+                take_larger(t)
+            nc.scalar.copy(win[t][:, :S], bank[:])
 
         out_rows = out.rearrange("(p t) j -> p t j", t=PACK)
-        larger = keep.tile([P, PACK, S], F32, name="larger")
         smaller = keep.tile([P, PACK, S], F32, name="smaller")
         g5 = keep.tile([P, PACK, S], F32, name="g5")
         res = keep.tile([P, PACK, S], F32, name="res")
         for t in range(last):
             nc.vector.tensor_copy(g5[:, t, :], win[t][:].indirect(n5_t[:]))
-            nc.vector.tensor_tensor(larger[:, t, :], g6[t], a_bank[t][:], ALU.max)
+            take_larger(t + 1 if t > 0 else 0)
             nc.vector.tensor_tensor(smaller[:, t, :], g5[:, t, :], b_bank[t][:], ALU.min)
             nc.gpsimd.tensor_tensor(res[:, t, :], larger[:, t, :], smaller[:, t, :], ALU.subtract)
             nc.sync.dma_start(out_rows[:, t, :], res[:, t, :])
-        nc.vector.tensor_tensor(larger[:, last, :], g6[last], a_bank[last][:], ALU.max)
         for cols in halves:
             nc.vector.tensor_copy(g5[:, last, cols], win[last][:].indirect(n5_t[:, cols.start // 16 : cols.stop // 16]))
         for cols in halves:

from contextlib import ExitStack

import concourse.mybir as mybir

K, T, S, N, H = 512, 2048, 512, 512, 512
FLOPS = 2 * S * (K * H + 2 * H * N)

F32 = mybir.dt.float32
BF16 = mybir.dt.bfloat16
I32 = mybir.dt.int32
U32 = mybir.dt.uint32
U16 = mybir.dt.uint16
U8 = mybir.dt.uint8
FP8X4 = mybir.dt.float8_e4m3fn_x4
ALU = mybir.AluOpType
ACT = mybir.ActivationFunctionType

P = 128
PACK = 4


def tile_picked_forkmaxbfracwind_none_p_kernel(
    tc, x_words, x_scales, w1, gn, w2, gm, w3, offs, n1, n2, n3, n4, n5, n6, out
):
    nc = tc.nc
    with ExitStack() as ctx:
        lists = ctx.enter_context(tc.tile_pool(name="lists", bufs=1))
        keep = ctx.enter_context(tc.tile_pool(name="keep", bufs=1))
        psum = ctx.enter_context(tc.psum_pool(name="psum", bufs=1))

        def load_list(name, src):
            tile = lists.tile([P, S // 16], U16, name=name)
            nc.sync.dma_start(tile[:], src)
            return tile

        def load_weight(name, src, tag):
            raw = keep.tile([P, PACK, H], F32, name=name, tag=tag, align_bytes=64)
            nc.sync.dma_start(raw[:], src.rearrange("(p j) c -> p j c", j=PACK))
            return raw

        def deal_weight(grouped, raw, shares):
            dst = grouped[:].rearrange("p (t m j) -> p m j t", t=PACK, j=PACK)
            src = raw[:].rearrange("p j (m t) -> p m j t", t=PACK)
            for engine_copy, lo, hi in shares:
                engine_copy(out=dst[:, lo:hi], in_=src[:, lo:hi])

        def quantise(name, grouped, tag=None):
            codes = keep.tile([P, S], U32, name=name + "_codes", tag=tag or name + "_codes", align_bytes=64)
            scales = keep.tile([P, S], U8, name=name + "_scales", align_bytes=64)
            nc.vector.quantize_mx(out=codes[:].bitcast(FP8X4), scales=scales[:], in_=grouped[:])
            return codes, scales

        def product(bank, weight, t, moving, places=slice(0, S)):
            cols = slice(t * P, (t + 1) * P)
            nc.tensor.matmul_mx(
                out=bank[:, places],
                lhsT=weight[0][:, cols].bitcast(FP8X4),
                lhsT_scale=weight[1][:, cols],
                rhs=moving[0][:, places].bitcast(FP8X4),
                rhs_scale=moving[1][:, places],
                start=True,
                stop=True,
            )

        def interleave(grouped, planes, sign):
            nc.scalar.activation(
                out=grouped[:].rearrange("p (c i t) -> p c t i", i=4, t=PACK),
                in_=planes[:].rearrange("p t (c i) -> p c t i", i=4),
                func=ACT.Copy,
                scale=sign,
            )

        xs = keep.tile([P, T], U8, name="xs", tag="xs", align_bytes=64)
        nc.gpsimd.memset(xs[:, : T // 2].bitcast(I32), 0)
        nc.vector.memset(xs[:, T // 2 :].bitcast(I32), 0)
        w1_raw = load_weight("w1_raw", w1, "w1_raw")
        offs_t = load_list("offs_t", offs)
        for r in range(4):
            nc.sync.dma_start(xs[r:P:32, :].bitcast(I32), x_scales[0, r:16:4, :].bitcast(I32))
        xw = keep.tile([P, T], I32, name="xw", tag="big", align_bytes=64)
        nc.sync.dma_start(xw[:], x_words[0].rearrange("p n r -> p (n r)").bitcast(I32))
        n4_t = load_list("n4_t", n4)
        n2_t = load_list("n2_t", n2)
        n3_t = load_list("n3_t", n3)
        gm_t = keep.tile([P, PACK], F32, name="gm_t")
        nc.sync.dma_start(gm_t[:], gm.rearrange("(p t) o -> p (t o)", t=PACK))
        gn_t = keep.tile([P, PACK], F32, name="gn_t")
        nc.sync.dma_start(gn_t[:], gn.rearrange("(p t) o -> p (t o)", t=PACK))
        n1_t = load_list("n1_t", n1)
        n6_t = load_list("n6_t", n6)
        n5_t = load_list("n5_t", n5)

        half = keep.tile([P, 1], F32, name="half")
        nc.vector.memset(half[:], 0.5)
        warm = keep.tile([P, 1], F32, name="warm")
        nc.scalar.activation(warm[:], half[:], ACT.Abs_reciprocal_sqrt)
        win = [keep.tile([P, 2 * S], F32, name=f"win{t}") for t in range(PACK)]
        bwin = [keep.tile([P, 2 * S], F32, name=f"bwin{t}") for t in range(PACK)]
        for t in range(PACK):
            nc.vector.memset(win[t][:, S:], 0.0)

        xq_scales = keep.tile([P, S], U8, name="xq_scales", align_bytes=64)
        nc.vector.tensor_copy(xq_scales[:], xs[:].indirect(offs_t[:]))
        w1_bf, w3_bf = [keep.tile([P, PACK * H], BF16, name=f"w{i}_bf", align_bytes=64) for i in (1, 3)]
        deal_weight(w1_bf, w1_raw, [(nc.scalar.copy, 0, 80), (nc.vector.tensor_copy, 80, P)])
        w1_q = quantise("w1", w1_bf, "xs")
        xq_words = keep.tile([P, S], U32, name="xq_words", align_bytes=64)
        halves = [slice(0, S // 2), slice(S // 2, S)]
        for cols in halves:
            nc.vector.tensor_copy(xq_words[:, cols], xw[:].bitcast(U32).indirect(offs_t[:, cols.start // 16 : cols.stop // 16]))
        w3_raw = load_weight("w3_raw", w3, "w1_raw")
        w2_raw = load_weight("w2_raw", w2, "big")

        last = PACK - 1
        y_plain = [bwin[t][:, S:] for t in range(PACK)]
        y_gm = keep.tile([P, last, S], F32, name="y_gm")
        early_bank = psum.tile([P, S], F32, name="early_bank", tag="second0")
        for t in range(PACK):
            bank = psum.tile([P, S], F32, name=f"y_bank{t}", tag=f"first{t}")
            parts = [(early_bank, halves[0]), (bank, halves[1])] if t == 0 else [(bank, slice(0, S))]
            for part, cols in parts:
                product(part, w1_q, t, (xq_words, xq_scales), cols)
                nc.scalar.copy(win[t][:, cols], part[:, cols])
            for part, cols in parts:
                nc.scalar.copy(y_plain[t][:, cols], part[:, cols])
            if t < last:
                for part, cols in parts:
                    nc.scalar.activation(y_gm[:, t, cols], part[:, cols], ACT.Copy, scale=gm_t[:, t : t + 1])

        recip = [keep.tile([P, S], F32, name=f"recip{t}")[:] for t in range(PACK)]
        z2 = keep.tile([P, PACK, S], F32, name="z2", tag="z2", align_bytes=64)
        for t in range(PACK):
            g4 = keep.tile([P, S], F32, name=f"g4_{t}", tag="g4", bufs=2)
            nc.vector.tensor_copy(g4[:], win[t][:].indirect(n4_t[:]))
            nc.vector.tensor_tensor(recip[t], win[t][:].indirect(n2_t[:]), y_plain[t], ALU.subtract)
            d3 = keep.tile([P, S], F32, name=f"d3_{t}", tag=f"d3_{t}", align_bytes=64)
            nc.vector.tensor_tensor(d3[:], win[t][:].indirect(n3_t[:]), g4[:], ALU.subtract)
            if t < last:
                nc.gpsimd.tensor_tensor(z2[:, t, :], d3[:], y_gm[:, t, :], ALU.mult)
            nc.scalar.activation(recip[t], recip[t], ACT.Abs)
            nc.scalar.activation(recip[t], recip[t], ACT.Abs_reciprocal_sqrt, bias=half[:])
            nc.scalar.activation(recip[t], recip[t], ACT.Square)
            if t == 0:
                deal_weight(w3_bf, w3_raw, [(nc.scalar.copy, 0, P)])

        z = keep.tile([P, PACK, S], F32, name="z", tag="d3_3", align_bytes=64)

        def z_gather(t, e1):
            nc.vector.tensor_tensor(e1, win[t][:].indirect(n1_t[:]), y_plain[t], ALU.subtract)

        def z_product(t, e1):
            nc.vector.scalar_tensor_tensor(z[:, t, :], e1, gn_t[:, t : t + 1], recip[t], ALU.mult, ALU.mult)

        e1 = [keep.tile([P, S], F32, name="e1_0", tag="d3_2", align_bytes=64)[:], z[:, 1, :]]
        z_gather(0, e1[0])
        nc.vector.scalar_tensor_tensor(z2[:, last, :], d3[:], gm_t[:, last:], y_plain[last], ALU.mult, ALU.mult)
        z2_bf = keep.tile([P, PACK * S], BF16, name="z2_bf", tag="z2_bf", align_bytes=64)
        interleave(z2_bf, z2, 1.0)
        w2_bf = keep.tile([P, PACK * H], BF16, name="w2_bf", tag="z2", align_bytes=64)
        deal_weight(w2_bf, w2_raw, [(nc.scalar.copy, 0, P)])
        z_product(0, e1[0])
        z_gather(1, e1[1])
        w3_q = quantise("w3", w3_bf, "d3_2")
        z_product(1, e1[1])
        z2_q = quantise("z2", z2_bf)
        b_bank = []
        for t in range(PACK):
            bank = psum.tile([P, S], F32, name=f"b_bank{t}", tag=f"second{t}")
            product(bank, w3_q, t, z2_q)
            nc.scalar.copy(bwin[t][:, :S], bank[:])
            b_bank.append(bank)
        e1_last = keep.tile([P, 2, S], F32, name="e1_last", tag="z2_bf", align_bytes=64)
        e1.extend([e1_last[:, 0, :], e1_last[:, 1, :]])
        z_gather(2, e1[2])
        z_gather(3, e1[3])
        z_product(2, e1[2])
        z_product(3, e1[3])
        z_bf = keep.tile([P, PACK * S], BF16, name="z_bf", tag="z_bf", align_bytes=64)
        interleave(z_bf, z, -1.0)
        w2_q = quantise("w2", w2_bf)

        g6_first = keep.tile([P, 3, S], F32, name="g6_first")
        for t in range(3):
            nc.vector.tensor_copy(g6_first[:, t, :], bwin[t][:].indirect(n6_t[:]))
        z_q = quantise("z", z_bf)
        g6_last = keep.tile([P, S], F32, name="g6_last", tag="z_bf", align_bytes=64)
        nc.vector.tensor_copy(g6_last[:], bwin[3][:].indirect(n6_t[:]))
        g6 = [g6_first[:, 0, :], g6_first[:, 1, :], g6_first[:, 2, :], g6_last[:]]
        larger = keep.tile([P, PACK, S], F32, name="larger")
        a_bank = []

        def take_larger(t):
            nc.vector.tensor_tensor(larger[:, t, :], g6[t], a_bank[t][:], ALU.max)

        for t in range(PACK):
            bank = psum.tile([P, S], F32, name=f"a_bank{t}", tag=f"first{t}")
            product(bank, w2_q, t, z_q)
            a_bank.append(bank)
            if t == 1:
                take_larger(t)
            nc.scalar.copy(win[t][:, :S], bank[:])

        out_rows = out.rearrange("(p t) j -> p t j", t=PACK)
        smaller = keep.tile([P, PACK, S], F32, name="smaller")
        g5 = keep.tile([P, PACK, S], F32, name="g5")
        res = keep.tile([P, PACK, S], F32, name="res")
        for t in range(last):
            nc.vector.tensor_copy(g5[:, t, :], win[t][:].indirect(n5_t[:]))
            take_larger(t + 1 if t > 0 else 0)
            nc.vector.tensor_tensor(smaller[:, t, :], g5[:, t, :], b_bank[t][:], ALU.min)
            nc.gpsimd.tensor_tensor(res[:, t, :], larger[:, t, :], smaller[:, t, :], ALU.subtract)
            nc.sync.dma_start(out_rows[:, t, :], res[:, t, :])
        for cols in halves:
            nc.vector.tensor_copy(g5[:, last, cols], win[last][:].indirect(n5_t[:, cols.start // 16 : cols.stop // 16]))
        for cols in halves:
            nc.vector.tensor_tensor(smaller[:, last, cols], g5[:, last, cols], b_bank[last][:, cols], ALU.min)
        for cols in halves:
            nc.vector.tensor_tensor(res[:, last, cols], larger[:, last, cols], smaller[:, last, cols], ALU.subtract)
            nc.sync.dma_start(out_rows[:, last, cols], res[:, last, cols])
